import numpy as np
import ml_dtypes


def mxq(x, axis, fmt="e4m3"):
    dtype, down = {"e4m3": (ml_dtypes.float8_e4m3fn, 7), "e5m2": (ml_dtypes.float8_e5m2, 14)}[fmt]
    v = np.moveaxis(np.asarray(x, np.float32).astype(ml_dtypes.bfloat16).astype(np.float64), axis, -1)
    blocks = v.reshape(v.shape[:-1] + (-1, 32))
    amax = np.abs(blocks).max(-1, keepdims=True)
    byte = np.maximum(np.where(amax > 0, np.frexp(amax)[1] - 1 + 127, 0) - down, 1)
    scale = np.exp2(byte - 127.0)
    codes = (blocks / scale).astype(np.float32).astype(dtype).astype(np.float64)
    return np.moveaxis((codes * scale).reshape(v.shape), -1, axis)


WIDE = False


def mx_kscale(k):
    if not WIDE:
        return np.ones(k)
    levels = np.array([10, -10, 5, -5, 0])
    if k % 512:
        return np.exp2(np.random.permutation(np.resize(levels, k // 32))).repeat(32)
    a = np.empty((k // 512, 16))
    for p in range(k // 512):
        a[p, :8] = np.random.permutation(np.resize(levels, 8))
        for g in range(8):
            far = levels[np.abs(levels - a[p, g]) >= 10]
            a[p, g + 8] = far[np.random.randint(len(far))]
    return np.exp2(a.ravel()).repeat(32)


def f64(x):
    return np.asarray(x).astype(np.float64)


def striped(idx):
    return np.tile(idx.reshape(-1, 16).T, (8, 1)).astype(np.uint16)


def unstriped(offs):
    return offs[:16].T.reshape(-1).astype(np.int64)


def striped8(idx):
    return np.concatenate([x.reshape(-1, 16).T for x in idx]).astype(np.uint16)


def runs(offs, k):
    lists = np.stack([offs[16 * r : 16 * r + 16].T.reshape(-1) for r in range(8)]).astype(np.int64)
    return lists[np.arange(k) % 512 // 64]


def pack_weight(w):
    k, n = w.shape
    w = f64(np.asarray(w, np.float32).astype(ml_dtypes.bfloat16)).reshape(k // 32, 32, n)
    amax = np.abs(w).max(1)
    byte = np.clip(np.where(amax > 0, np.frexp(amax)[1] - 1 + 127 - 7, 1), 1, 254)
    scaled = (w * np.exp2(127.0 - byte)[:, None, :]).reshape(k, n).astype(np.float32)
    words = np.ascontiguousarray(scaled.reshape(k // 512, 128, 4, n).transpose(0, 1, 3, 2)).astype(ml_dtypes.float8_e4m3fn).view(np.uint8)
    return words, np.ascontiguousarray(byte.astype(np.uint8).reshape(k // 512, 16, n))


def unpack_weight(words, scales):
    g, p, n, _ = words.shape
    vals = np.ascontiguousarray(words).view(ml_dtypes.float8_e4m3fn).astype(np.float64) * np.repeat(np.exp2(scales.astype(np.float64) - 127.0), 8, axis=1)[..., None]
    return vals.transpose(0, 1, 3, 2).reshape(g * 512, n)

def planes(y):
    n, m = y.shape
    v = y.astype(np.float32).astype(ml_dtypes.bfloat16).astype(np.float64).reshape(n // 32, 32, m)
    top = np.abs(v).max(1)
    byte = np.clip(np.where(top > 0, np.frexp(top)[1] - 1 + 127 - 7, 1), 1, 254)
    codes = (v * np.exp2(127.0 - byte)[:, None, :]).reshape(n, m).astype(np.float32).astype(ml_dtypes.float8_e4m3fn).view(np.uint8)
    words = codes.reshape(n // 512, 128, 4, m).transpose(0, 1, 3, 2)
    return np.ascontiguousarray(words), np.ascontiguousarray(byte.astype(np.uint8).reshape(n // 512, 16, m))


K, T, S, N, H, J = 512, 2048, 512, 512, 512, 512


def setup_inputs():
    n = np.random.standard_normal
    s = mx_kscale(K)[:, None]
    u = mx_kscale(S)
    packed_xT = pack_weight(n((K, T)) * s)
    packed_w1 = pack_weight(n((S, N)) / np.sqrt(S) / u[:, None])
    return {
        "x_words": packed_xT[0],
        "x_scales": packed_xT[1],
        "wa": (n((K, H)) / np.sqrt(K) / s).astype(np.float32),
        "gt": (np.random.uniform(0.5, 1.5, (S, 1)) * u[:, None]).astype(np.float32),
        "w1_words": packed_w1[0],
        "w1_scales": packed_w1[1],
        "tab": n((N, J)).astype(np.float32),
        "offs": striped(np.random.permutation(T)[:S]),
        "n1": striped8(np.stack([np.random.permutation(H) for _ in range(8)])),
        "n2": striped8(np.stack([np.random.permutation(H) for _ in range(8)])),
        "n3": striped8(np.random.randint(0, J, (8, H))),
        "n4": striped8(np.stack([np.random.permutation(H) for _ in range(8)])),
    }


def reference(x_words, x_scales, wa, gt, w1_words, w1_scales, tab, offs, n1, n2, n3, n4):
    xq = unpack_weight(x_words, x_scales)[:, unstriped(offs)]
    y = xq.T @ mxq(f64(wa), 0, "e4m3")
    z = f64(gt) * ((np.tanh(y[np.arange(S)[:, None], runs(n1, S)] - y)) * (y[np.arange(S)[:, None], runs(n2, S)]))
    h = unpack_weight(w1_words, w1_scales).T @ mxq(z, 0, "e4m3")
    out_0 = np.maximum(h + f64(tab)[np.arange(N)[:, None], runs(n3, N)], h[np.arange(N)[:, None], runs(n4, N)])
    return (out_0,) + planes(out_0)

@@ -1,0 +1,200 @@
+from contextlib import ExitStack
+
+import concourse.mybir as mybir
+
+K, T, S, N, H, J = 512, 2048, 512, 512, 512, 512
+FLOPS = 2 * K * S * H + 2 * S * N * H
+
+F32 = mybir.dt.float32
+BF16 = mybir.dt.bfloat16
+I32 = mybir.dt.int32
+U32 = mybir.dt.uint32
+U16 = mybir.dt.uint16
+U8 = mybir.dt.uint8
+FP8X4 = mybir.dt.float8_e4m3fn_x4
+ALU = mybir.AluOpType
+ACT = mybir.ActivationFunctionType
+
+P = 128
+PACK = 4
+HALF = 256
+LANES = 16
+
+
+def tile_picked_tokfdifkind_none_po_kernel(tc, x_words, x_scales, wa, gt, w1_words, w1_scales, tab, offs, n1, n2, n3, n4, out_0, out_1, out_2):
+    nc = tc.nc
+    with ExitStack() as ctx:
+        keep = ctx.enter_context(tc.tile_pool(name="keep", bufs=1))
+        psum = ctx.enter_context(tc.psum_pool(name="psum", bufs=1))
+
+        def tile(name, shape, dtype):
+            return keep.tile(shape, dtype, name=name, align_bytes=64)
+
+        def load_list(name, src):
+            t = tile(name, [P, H // LANES], U16)
+            nc.sync.dma_start(t[:], src)
+            return t
+
+        def entries(lst, c0, c1):
+            return lst[:, c0 // LANES : c1 // LANES]
+
+        def load_scales(queue, dst, src):
+            for q in range(4):
+                queue.dma_start(dst[32 * q : 32 * q + 4, :].bitcast(I32), src[0, 4 * q : 4 * q + 4, :].bitcast(I32))
+
+        def load_words(dst, src):
+            nc.sync.dma_start(dst[:], src[0].rearrange("p n t -> p (n t)").bitcast(I32))
+
+        def deal(name, src, dtype):
+            dst = tile(name, [P, S], dtype)
+            nc.vector.tensor_copy(dst[:].rearrange("p (t m) -> p t m", t=PACK), src.rearrange("p (m t) -> p t m", t=PACK))
+            return dst
+
+        def interleave(copy, dst, src):
+            copy(dst.rearrange("p (c i t) -> p c t i", i=4, t=PACK), src.rearrange("p t (c i) -> p c t i", i=4))
+
+        xs_all = tile("xs_all", [P, T], U8)
+        ws_raw = tile("ws_raw", [P, N], U8)
+        nc.vector.memset(xs_all[:].bitcast(I32), 0)
+        nc.vector.memset(ws_raw[:].bitcast(I32), 0)
+
+        offs_t = load_list("offs_t", offs)
+        gt_t = tile("gt_t", [P, PACK], F32)
+        nc.scalar.dma_start(gt_t[:], gt.rearrange("(p t) o -> p (t o)", t=PACK))
+        n1_t = load_list("n1_t", n1)
+        n2_t = load_list("n2_t", n2)
+        n3_t = load_list("n3_t", n3)
+        n4_t = load_list("n4_t", n4)
+        warm = tile("warm", [P, 1], F32)
+        nc.scalar.activation(warm[:], gt_t[:, 0:1], ACT.Tanh)
+        wa_rows = wa.rearrange("(p j) c -> p j c", j=PACK)
+        wa_cols = [(0, 128), (128, 384), (384, 512)]
+        wa_raw = [tile("wa_raw%d" % a, [P, PACK, c1 - c0], F32) for a, (c0, c1) in enumerate(wa_cols)]
+        xw_all = tile("xw_all", [P, T], I32)
+        load_scales(nc.sync, xs_all, x_scales)
+        load_words(xw_all, x_words)
+        for a, (c0, c1) in enumerate(wa_cols):
+            nc.sync.dma_start(wa_raw[a][:], wa_rows[:, :, c0:c1])
+        ww_raw = tile("ww_raw", [P, N], I32)
+        load_words(ww_raw, w1_words)
+        load_scales(nc.sync, ws_raw, w1_scales)
+        tab_rows = tab.rearrange("(p t) c -> p t c", t=PACK)
+        tab_t = []
+        for t in range(PACK):
+            rows = tile("tab%d" % t, [P, 2 * J], F32)
+            nc.sync.dma_start(rows[:, :J], tab_rows[:, t, :])
+            tab_t.append(rows)
+
+        y = [tile("y%d" % t, [P, 2 * H], F32) for t in range(PACK)]
+        def quantize(name, grouped, width):
+            codes = tile(name + "_codes", [P, width], U32)
+            scales = tile(name + "_scales", [P, width], U8)
+            nc.vector.quantize_mx(codes[:].bitcast(FP8X4), scales[:], grouped)
+            return codes, scales
+
+        def product(out, t, words, scales, quantized):
+            rows = slice(t * P, (t + 1) * P)
+            nc.tensor.matmul_mx(out, lhsT=words[:, rows].bitcast(FP8X4), lhsT_scale=scales[:, rows],
+                                rhs=quantized[0][:].bitcast(FP8X4), rhs_scale=quantized[1][:], start=True, stop=True)
+
+        cols = [slice(0, HALF), slice(HALF, H)]
+        y_ps = [psum.tile([P, H], F32, name="y_ps%d" % t) for t in range(PACK)]
+        wa_bf = [tile("wa_bf%d" % a, [P, PACK * (c1 - c0)], BF16) for a, (c0, c1) in enumerate(wa_cols)]
+        xw_pick = tile("xw_pick", [P, S], U32)
+        nc.vector.tensor_copy(xw_pick[:], xw_all[:].bitcast(U32).indirect(offs_t[:]))
+        xs_pick = tile("xs_pick", [P, S], U8)
+        nc.vector.tensor_copy(xs_pick[:], xs_all[:].indirect(offs_t[:]))
+        xw = deal("xw", xw_pick[:], U32)
+        xs = deal("xs", xs_pick[:], U8)
+        wa_q = {}
+        for a in (0, 2, 1):
+            interleave(nc.vector.tensor_copy if a == 2 else nc.scalar.copy, wa_bf[a][:], wa_raw[a][:])
+        for a in (0, 2, 1):
+            wa_q[a] = quantize("wa%d" % a, wa_bf[a][:], wa_cols[a][1] - wa_cols[a][0])
+        for t in range(PACK):
+            for a in (0, 2, 1):
+                product(y_ps[t][:, wa_cols[a][0] : wa_cols[a][1]], t, xw, xs, wa_q[a])
+        ww = deal("ww", ww_raw[:].bitcast(U32), U32)
+
+        gy = [tile("gy%d" % t, [P, 2 * H], F32) for t in range(PACK)]
+        diff = [tile("diff%d" % t, [P, H], F32) for t in range(PACK)]
+        th = [tile("th%d" % t, [P, H], F32) for t in range(PACK)]
+        z = tile("z", [P, PACK, H], F32)
+
+        def Y(t):
+            nc.scalar.copy(y[t][:, :H], y_ps[t][:])
+
+        def O(t):
+            nc.scalar.copy(gy[t][:, H:], y_ps[t][:])
+
+        def G(t):
+            nc.scalar.activation(gy[t][:, :H], y_ps[t][:], ACT.Copy, scale=gt_t[:, t : t + 1])
+
+        def D(t):
+            nc.vector.tensor_tensor(diff[t][:], y[t][:].indirect(n1_t[:]), gy[t][:, H:], ALU.subtract)
+
+        def TH(t, c0=0, c1=H):
+            nc.scalar.activation(th[t][:, c0:c1], diff[t][:, c0:c1], ACT.Tanh)
+
+        def M(t, c0=0, c1=H):
+            nc.vector.tensor_tensor(z[:, t, c0:c1], gy[t][:].indirect(entries(n2_t, c0, c1)), th[t][:, c0:c1], ALU.mult)
+
+        Y(0)
+        nc.vector.tensor_copy(gy[0][:, H:], y[0][:, :H])
+        D(0)
+        ws = deal("ws", ws_raw[:], U8)
+        G(0); Y(1); O(1); D(1); TH(0); M(0); G(1); Y(2); TH(1); M(1); O(2); D(2); Y(3); O(3); D(3); G(2); G(3)
+        TH(2, 0, HALF); M(2, 0, HALF); TH(2, HALF, H); TH(3, 0, HALF); M(3, 0, HALF); TH(3, HALF, H)
+        z_bf = [tile("z_bf%d" % a, [P, PACK * HALF], BF16) for a in range(2)]
+        interleave(nc.scalar.copy, z_bf[0][:], z[:, :, cols[0]])
+        M(2, HALF, H); M(3, HALF, H)
+        h_ps = [[psum.tile([P, HALF], F32, name="h_ps%d" % t)[:] for t in range(PACK)], [y_ps[t][:, :HALF] for t in range(PACK)]]
+
+        def second_product(a):
+            quantized = quantize("z%d" % a, z_bf[a][:], HALF)
+            for t in range(PACK):
+                product(h_ps[a][t], t, ww, ws, quantized)
+
+        h = y
+
+        def HC(t, a):
+            nc.scalar.copy(h[t][:, cols[a]], h_ps[a][t])
+
+        second_product(0)
+        interleave(nc.scalar.copy, z_bf[1][:, : 2 * HALF], z[:, :, 256:384])
+        interleave(nc.vector.tensor_copy, z_bf[1][:, 2 * HALF :], z[:, :, 384:512])
+        second_product(1)
+        HC(0, 0); HC(1, 0); HC(0, 1); HC(1, 1); HC(2, 0); HC(2, 1); HC(3, 0); HC(3, 1)
+
+        out_rows = out_0.rearrange("(p t) c -> p t c", t=PACK)
+        out_words = out_1[0].rearrange("p n t -> p (n t)").bitcast(I32)
+        o_codes = tile("o_codes", [P, H], I32)
+        o_scales = tile("o_scales", [P, H], U8)
+        first = [tile("first%d" % t, [P, H], F32) for t in range(PACK)]
+        second = [tile("second%d" % t, [P, H], F32) for t in range(PACK)]
+        res = tile("res", [P, PACK, H], F32)
+        res_bf = tile("res_bf", [P, PACK * H], BF16)
+
+        def A(t, c0=0, c1=H):
+            nc.vector.tensor_tensor(first[t][:, c0:c1], tab_t[t][:].indirect(entries(n3_t, c0, c1)), h[t][:, c0:c1], ALU.add)
+
+        def B(t, c0=0, c1=H):
+            nc.vector.tensor_copy(second[t][:, c0:c1], h[t][:].indirect(entries(n4_t, c0, c1)))
+
+        def X(t, c0=0, c1=H):
+            nc.vector.tensor_tensor(res[:, t, c0:c1], first[t][:, c0:c1], second[t][:, c0:c1], ALU.max)
+            nc.sync.dma_start(out_rows[:, t, c0:c1], res[:, t, c0:c1])
+
+        def R(copy, c0, c1):
+            interleave(copy, res_bf[:, PACK * c0 : PACK * c1], res[:, :, c0:c1])
+
+        def Q(c0, c1):
+            nc.vector.quantize_mx(o_codes[:, c0:c1].bitcast(FP8X4), o_scales[:, c0:c1], res_bf[:, PACK * c0 : PACK * c1])
+            nc.sync.dma_start(out_words[:, c0:c1], o_codes[:, c0:c1])
+
+        A(0, 0, HALF); B(0); A(0, HALF, H); A(1); X(0); B(1); A(2); X(1); B(2); A(3, 0, HALF)
+        B(3, 0, HALF); X(2); X(3, 0, HALF); R(nc.scalar.copy, 0, 256); A(3, HALF, H); B(3, HALF, H); X(3, HALF, H)
+        R(nc.scalar.copy, 256, 384); Q(0, 256); R(nc.vector.tensor_copy, 384, 512); Q(256, 512)
+        for q in range(4):
+            queue = nc.scalar if q % 2 else nc.sync
+            queue.dma_start(out_2[0, 4 * q : 4 * q + 4, :].bitcast(I32), o_scales[32 * q : 32 * q + 4, :].bitcast(I32))

@@ -27,8 +27,8 @@ def tile_picked_tokfdifkind_none_po_kernel(tc, x_words, x_scales, wa, gt, w1_wor
         keep = ctx.enter_context(tc.tile_pool(name="keep", bufs=1))
         psum = ctx.enter_context(tc.psum_pool(name="psum", bufs=1))
 
-        def tile(name, shape, dtype):
-            return keep.tile(shape, dtype, name=name, align_bytes=64)
+        def tile(name, shape, dtype, tag=None):
+            return keep.tile(shape, dtype, name=name, tag=tag or name, align_bytes=64)
 
         def load_list(name, src):
             t = tile(name, [P, H // LANES], U16)
@@ -45,76 +45,82 @@ def tile_picked_tokfdifkind_none_po_kernel(tc, x_words, x_scales, wa, gt, w1_wor
         def load_words(dst, src):
             nc.sync.dma_start(dst[:], src[0].rearrange("p n t -> p (n t)").bitcast(I32))
 
-        def deal(name, src, dtype):
-            dst = tile(name, [P, S], dtype)
+        def deal(name, src, dtype, tag=None):
+            dst = tile(name, [P, S], dtype, tag)
             nc.vector.tensor_copy(dst[:].rearrange("p (t m) -> p t m", t=PACK), src.rearrange("p (m t) -> p t m", t=PACK))
             return dst
 
         def interleave(copy, dst, src):
             copy(dst.rearrange("p (c i t) -> p c t i", i=4, t=PACK), src.rearrange("p t (c i) -> p c t i", i=4))
 
+        def shared(dst, src, share):
+            interleave(nc.scalar.copy, dst[:, : PACK * share], src[:, :, :share])
+            interleave(nc.vector.tensor_copy, dst[:, PACK * share :], src[:, :, share:])
+
         xs_all = tile("xs_all", [P, T], U8)
-        ws_raw = tile("ws_raw", [P, N], U8)
-        nc.vector.memset(xs_all[:].bitcast(I32), 0)
-        nc.vector.memset(ws_raw[:].bitcast(I32), 0)
+        nc.vector.memset(xs_all[:, : T // 2].bitcast(I32), 0)
+        nc.gpsimd.memset(xs_all[:, T // 2 :].bitcast(I32), 0)
+        warm_in = tile("warm_in", [P, 1], F32, "wa_raw0")
+        warm_out = tile("warm_out", [P, 1], F32, "wa_raw1")
+        nc.vector.memset(warm_in[:], 0.0)
+        nc.scalar.activation(warm_out[:], warm_in[:], ACT.Tanh)
 
         offs_t = load_list("offs_t", offs)
-        gt_t = tile("gt_t", [P, PACK], F32)
-        nc.scalar.dma_start(gt_t[:], gt.rearrange("(p t) o -> p (t o)", t=PACK))
         n1_t = load_list("n1_t", n1)
         n2_t = load_list("n2_t", n2)
+        load_scales(nc.sync, xs_all, x_scales)
+        xw_all = tile("xw_all", [P, T], I32)
+        load_words(xw_all, x_words)
         n3_t = load_list("n3_t", n3)
         n4_t = load_list("n4_t", n4)
-        warm = tile("warm", [P, 1], F32)
-        nc.scalar.activation(warm[:], gt_t[:, 0:1], ACT.Tanh)
         wa_rows = wa.rearrange("(p j) c -> p j c", j=PACK)
-        wa_cols = [(0, 128), (128, 384), (384, 512)]
-        wa_raw = [tile("wa_raw%d" % a, [P, PACK, c1 - c0], F32) for a, (c0, c1) in enumerate(wa_cols)]
-        xw_all = tile("xw_all", [P, T], I32)
-        load_scales(nc.sync, xs_all, x_scales)
-        load_words(xw_all, x_words)
-        for a, (c0, c1) in enumerate(wa_cols):
-            nc.sync.dma_start(wa_raw[a][:], wa_rows[:, :, c0:c1])
-        ww_raw = tile("ww_raw", [P, N], I32)
-        load_words(ww_raw, w1_words)
-        load_scales(nc.sync, ws_raw, w1_scales)
-        tab_rows = tab.rearrange("(p t) c -> p t c", t=PACK)
-        tab_t = []
-        for t in range(PACK):
-            rows = tile("tab%d" % t, [P, 2 * J], F32)
-            nc.sync.dma_start(rows[:, :J], tab_rows[:, t, :])
-            tab_t.append(rows)
+        wa_raw = [tile("wa_raw%d" % a, [P, PACK, HALF], F32) for a in range(2)]
+        for a in range(2):
+            nc.sync.dma_start(wa_raw[a][:], wa_rows[:, :, a * HALF : (a + 1) * HALF])
 
         y = [tile("y%d" % t, [P, 2 * H], F32) for t in range(PACK)]
-        def quantize(name, grouped, width):
-            codes = tile(name + "_codes", [P, width], U32)
-            scales = tile(name + "_scales", [P, width], U8)
-            nc.vector.quantize_mx(codes[:].bitcast(FP8X4), scales[:], grouped)
-            return codes, scales
+        def quantize(codes, scales, grouped):
+            nc.vector.quantize_mx(codes.bitcast(FP8X4), scales, grouped)
 
-        def product(out, t, words, scales, quantized):
+        def product(out, t, words, scales, codes, code_scales):
             rows = slice(t * P, (t + 1) * P)
             nc.tensor.matmul_mx(out, lhsT=words[:, rows].bitcast(FP8X4), lhsT_scale=scales[:, rows],
-                                rhs=quantized[0][:].bitcast(FP8X4), rhs_scale=quantized[1][:], start=True, stop=True)
+                                rhs=codes.bitcast(FP8X4), rhs_scale=code_scales, start=True, stop=True)
 
         cols = [slice(0, HALF), slice(HALF, H)]
         y_ps = [psum.tile([P, H], F32, name="y_ps%d" % t) for t in range(PACK)]
-        wa_bf = [tile("wa_bf%d" % a, [P, PACK * (c1 - c0)], BF16) for a, (c0, c1) in enumerate(wa_cols)]
-        xw_pick = tile("xw_pick", [P, S], U32)
-        nc.vector.tensor_copy(xw_pick[:], xw_all[:].bitcast(U32).indirect(offs_t[:]))
         xs_pick = tile("xs_pick", [P, S], U8)
         nc.vector.tensor_copy(xs_pick[:], xs_all[:].indirect(offs_t[:]))
-        xw = deal("xw", xw_pick[:], U32)
+        xw_pick = tile("xw_pick", [P, S], U32)
+        nc.vector.tensor_copy(xw_pick[:], xw_all[:].bitcast(U32).indirect(offs_t[:]))
         xs = deal("xs", xs_pick[:], U8)
-        wa_q = {}
-        for a in (0, 2, 1):
-            interleave(nc.vector.tensor_copy if a == 2 else nc.scalar.copy, wa_bf[a][:], wa_raw[a][:])
-        for a in (0, 2, 1):
-            wa_q[a] = quantize("wa%d" % a, wa_bf[a][:], wa_cols[a][1] - wa_cols[a][0])
-        for t in range(PACK):
-            for a in (0, 2, 1):
-                product(y_ps[t][:, wa_cols[a][0] : wa_cols[a][1]], t, xw, xs, wa_q[a])
-        ww = deal("ww", ww_raw[:].bitcast(U32), U32)
+        xw = deal("xw", xw_pick[:], U32)
+        wa_bf = [tile("wa_bf%d" % a, [P, PACK * HALF], BF16) for a in range(2)]
+        wa_codes = tile("wa_codes", [P, H], U32)
+        wa_scales = tile("wa_scales", [P, H], U8)
+        h_ps = [[psum.tile([P, HALF], F32, name="h_ps%d" % t)[:] for t in range(PACK)], [y_ps[t][:, :HALF] for t in range(PACK)]]
+        y0_ps = [h_ps[0][0], h_ps[1][0]]
+        for a, share in enumerate((128, 64)):
+            shared(wa_bf[a][:], wa_raw[a][:], share)
+            quantize(wa_codes[:, cols[a]], wa_scales[:, cols[a]], wa_bf[a][:])
+            product(y0_ps[a], 0, xw, xs, wa_codes[:, cols[a]], wa_scales[:, cols[a]])
+        for t in range(1, PACK):
+            product(y_ps[t][:], t, xw, xs, wa_codes[:], wa_scales[:])
+
+        gt_t = tile("gt_t", [P, PACK], F32, "xs_pick")
+        nc.sync.dma_start(gt_t[:], gt.rearrange("(p t) o -> p (t o)", t=PACK))
+        ww_raw = tile("ww_raw", [P, N], I32, "xw_all")
+        load_words(ww_raw, w1_words)
+        ws_raw = tile("ws_raw", [P, N], U8, "xs_all")
+        nc.gpsimd.memset(ws_raw[:].bitcast(I32), 0)
+        load_scales(nc.sync, ws_raw, w1_scales)
+        ww = deal("ww", ww_raw[:].bitcast(U32), U32, "wa_bf1")
+        tab_rows = tab.rearrange("(p t) c -> p t c", t=PACK)
+        tab_t = []
+        for t, tag in enumerate(("wa_raw0", "wa_raw1", "wa_bf0", "xw_all")):
+            rows = tile("tab%d" % t, [P, 2 * J], F32, tag)
+            nc.sync.dma_start(rows[:, :J], tab_rows[:, t, :])
+            tab_t.append(rows)
 
         gy = [tile("gy%d" % t, [P, 2 * H], F32) for t in range(PACK)]
         diff = [tile("diff%d" % t, [P, H], F32) for t in range(PACK)]
@@ -130,8 +136,8 @@ def tile_picked_tokfdifkind_none_po_kernel(tc, x_words, x_scales, wa, gt, w1_wor
         def G(t):
             nc.scalar.activation(gy[t][:, :H], y_ps[t][:], ACT.Copy, scale=gt_t[:, t : t + 1])
 
-        def D(t):
-            nc.vector.tensor_tensor(diff[t][:], y[t][:].indirect(n1_t[:]), gy[t][:, H:], ALU.subtract)
+        def D(t, c0=0, c1=H):
+            nc.vector.tensor_tensor(diff[t][:, c0:c1], y[t][:].indirect(entries(n1_t, c0, c1)), gy[t][:, H + c0 : H + c1], ALU.subtract)
 
         def TH(t, c0=0, c1=H):
             nc.scalar.activation(th[t][:, c0:c1], diff[t][:, c0:c1], ACT.Tanh)
@@ -139,21 +145,29 @@ def tile_picked_tokfdifkind_none_po_kernel(tc, x_words, x_scales, wa, gt, w1_wor
         def M(t, c0=0, c1=H):
             nc.vector.tensor_tensor(z[:, t, c0:c1], gy[t][:].indirect(entries(n2_t, c0, c1)), th[t][:, c0:c1], ALU.mult)
 
-        Y(0)
-        nc.vector.tensor_copy(gy[0][:, H:], y[0][:, :H])
-        D(0)
-        ws = deal("ws", ws_raw[:], U8)
-        G(0); Y(1); O(1); D(1); TH(0); M(0); G(1); Y(2); TH(1); M(1); O(2); D(2); Y(3); O(3); D(3); G(2); G(3)
-        TH(2, 0, HALF); M(2, 0, HALF); TH(2, HALF, H); TH(3, 0, HALF); M(3, 0, HALF); TH(3, HALF, H)
+        nc.scalar.copy(y[0][:, :HALF], y0_ps[0])
+        nc.scalar.copy(gy[0][:, H : H + HALF], y0_ps[0])
+        nc.scalar.copy(y[0][:, HALF:H], y0_ps[1])
+        D(0, 0, HALF)
+        nc.scalar.copy(gy[0][:, H + HALF :], y0_ps[1])
+        D(0, HALF, H)
+        Y(1); O(1); D(1)
+        for a in range(2):
+            nc.scalar.activation(gy[0][:, cols[a]], y0_ps[a], ACT.Copy, scale=gt_t[:, 0:1])
+        TH(0)
+        ws = deal("ws", ws_raw[:], U8, "diff0")
+        M(0); G(1); TH(1); M(1); Y(2); O(2); D(2); Y(3); O(3); D(3); G(2)
+        TH(2, 0, HALF); M(2, 0, HALF); G(3); TH(2, HALF, H); TH(3, 0, HALF); M(3, 0, HALF); TH(3, HALF, H)
         z_bf = [tile("z_bf%d" % a, [P, PACK * HALF], BF16) for a in range(2)]
         interleave(nc.scalar.copy, z_bf[0][:], z[:, :, cols[0]])
         M(2, HALF, H); M(3, HALF, H)
-        h_ps = [[psum.tile([P, HALF], F32, name="h_ps%d" % t)[:] for t in range(PACK)], [y_ps[t][:, :HALF] for t in range(PACK)]]
 
         def second_product(a):
-            quantized = quantize("z%d" % a, z_bf[a][:], HALF)
+            z_codes = tile("z_codes%d" % a, [P, HALF], U32)
+            z_scales = tile("z_scales%d" % a, [P, HALF], U8)
+            quantize(z_codes[:], z_scales[:], z_bf[a][:])
             for t in range(PACK):
-                product(h_ps[a][t], t, ww, ws, quantized)
+                product(h_ps[a][t], t, ww, ws, z_codes[:], z_scales[:])
 
         h = y
 
@@ -161,8 +175,7 @@ def tile_picked_tokfdifkind_none_po_kernel(tc, x_words, x_scales, wa, gt, w1_wor
             nc.scalar.copy(h[t][:, cols[a]], h_ps[a][t])
 
         second_product(0)
-        interleave(nc.scalar.copy, z_bf[1][:, : 2 * HALF], z[:, :, 256:384])
-        interleave(nc.vector.tensor_copy, z_bf[1][:, 2 * HALF :], z[:, :, 384:512])
+        shared(z_bf[1][:], z[:, :, cols[1]], 96)
         second_product(1)
         HC(0, 0); HC(1, 0); HC(0, 1); HC(1, 1); HC(2, 0); HC(2, 1); HC(3, 0); HC(3, 1)
 
@@ -170,31 +183,31 @@ def tile_picked_tokfdifkind_none_po_kernel(tc, x_words, x_scales, wa, gt, w1_wor
         out_words = out_1[0].rearrange("p n t -> p (n t)").bitcast(I32)
         o_codes = tile("o_codes", [P, H], I32)
         o_scales = tile("o_scales", [P, H], U8)
-        first = [tile("first%d" % t, [P, H], F32) for t in range(PACK)]
-        second = [tile("second%d" % t, [P, H], F32) for t in range(PACK)]
+        first = tile("first", [P, PACK, H], F32)
+        second = tile("second", [P, PACK, H], F32)
         res = tile("res", [P, PACK, H], F32)
         res_bf = tile("res_bf", [P, PACK * H], BF16)
 
         def A(t, c0=0, c1=H):
-            nc.vector.tensor_tensor(first[t][:, c0:c1], tab_t[t][:].indirect(entries(n3_t, c0, c1)), h[t][:, c0:c1], ALU.add)
+            nc.vector.tensor_tensor(first[:, t, c0:c1], tab_t[t][:].indirect(entries(n3_t, c0, c1)), h[t][:, c0:c1], ALU.add)
 
         def B(t, c0=0, c1=H):
-            nc.vector.tensor_copy(second[t][:, c0:c1], h[t][:].indirect(entries(n4_t, c0, c1)))
+            nc.vector.tensor_copy(second[:, t, c0:c1], h[t][:].indirect(entries(n4_t, c0, c1)))
 
-        def X(t, c0=0, c1=H):
-            nc.vector.tensor_tensor(res[:, t, c0:c1], first[t][:, c0:c1], second[t][:, c0:c1], ALU.max)
-            nc.sync.dma_start(out_rows[:, t, c0:c1], res[:, t, c0:c1])
-
-        def R(copy, c0, c1):
-            interleave(copy, res_bf[:, PACK * c0 : PACK * c1], res[:, :, c0:c1])
+        def X(t0, t1, c0=0, c1=H):
+            nc.vector.tensor_tensor(res[:, t0:t1, c0:c1], first[:, t0:t1, c0:c1], second[:, t0:t1, c0:c1], ALU.max)
+            nc.sync.dma_start(out_rows[:, t0:t1, c0:c1], res[:, t0:t1, c0:c1])
 
         def Q(c0, c1):
             nc.vector.quantize_mx(o_codes[:, c0:c1].bitcast(FP8X4), o_scales[:, c0:c1], res_bf[:, PACK * c0 : PACK * c1])
             nc.sync.dma_start(out_words[:, c0:c1], o_codes[:, c0:c1])
 
-        A(0, 0, HALF); B(0); A(0, HALF, H); A(1); X(0); B(1); A(2); X(1); B(2); A(3, 0, HALF)
-        B(3, 0, HALF); X(2); X(3, 0, HALF); R(nc.scalar.copy, 0, 256); A(3, HALF, H); B(3, HALF, H); X(3, HALF, H)
-        R(nc.scalar.copy, 256, 384); Q(0, 256); R(nc.vector.tensor_copy, 384, 512); Q(256, 512)
+        A(0, 0, HALF); A(1, 0, HALF); B(0); A(0, HALF, H); A(1, HALF, H); B(1); X(0, 1); A(2); X(1, 2); A(3)
+        B(2, 0, HALF); B(3, 0, HALF); B(2, HALF, H); X(2, 4, 0, HALF)
+        interleave(nc.scalar.copy, res_bf[:, : PACK * HALF], res[:, :, :HALF])
+        B(3, HALF, H); X(2, 3, HALF, H); X(3, 4, HALF, H); Q(0, HALF)
+        shared(res_bf[:, PACK * HALF :], res[:, :, HALF:], 64)
+        Q(HALF, H)
         for q in range(4):
             queue = nc.scalar if q % 2 else nc.sync
             queue.dma_start(out_2[0, 4 * q : 4 * q + 4, :].bitcast(I32), o_scales[32 * q : 32 * q + 4, :].bitcast(I32))

@@ -2,7 +2,7 @@ from contextlib import ExitStack
 
 import concourse.mybir as mybir
 
-K, T, S, N, H, J = 512, 2048, 512, 512, 512, 512
+K, T, S, N, H = 512, 2048, 512, 512, 512
 FLOPS = 2 * K * S * H + 2 * S * N * H
 
 F32 = mybir.dt.float32
@@ -17,197 +17,246 @@ ACT = mybir.ActivationFunctionType
 
 P = 128
 PACK = 4
-HALF = 256
-LANES = 16
+GROUP = 16
+QUADRANTS = 4
+WINDOW = 2 * H
+HALF, QUARTER = H // 2, H // 4
+HALVES = (slice(0, HALF), slice(HALF, H))
+QUARTERS = tuple(slice(c, c + QUARTER) for c in range(0, H, QUARTER))
+WHOLE = slice(0, H)
+WA_SCALAR_SHARE = 64
 
 
-def tile_picked_tokfdifkind_none_po_kernel(tc, x_words, x_scales, wa, gt, w1_words, w1_scales, tab, offs, n1, n2, n3, n4, out_0, out_1, out_2):
+def tile_picked_tokfdifkind_none_po_kernel(
+    tc, x_words, x_scales, wa, gt, w1_words, w1_scales, tab, offs, n1, n2, n3, n4, out_0, out_1, out_2
+):
     nc = tc.nc
     with ExitStack() as ctx:
         keep = ctx.enter_context(tc.tile_pool(name="keep", bufs=1))
         psum = ctx.enter_context(tc.psum_pool(name="psum", bufs=1))
 
-        def tile(name, shape, dtype, tag=None):
-            return keep.tile(shape, dtype, name=name, tag=tag or name, align_bytes=64)
+        def tile(name, shape, dtype, after=None):
+            return keep.tile(shape, dtype, name=name, tag=after or name, align_bytes=64)
+
+        def dealt(rows):
+            return rows.rearrange("(p t) c -> p t c", t=PACK)
+
+        def words_of(packed):
+            return packed[0].rearrange("p n t -> p (n t)").bitcast(I32)
+
+        def scale_rows(plane, q):
+            return plane[32 * q : 32 * q + 4, :].bitcast(I32)
+
+        def load(name, shape, dtype, src):
+            dst = tile(name, shape, dtype)
+            nc.sync.dma_start(dst[:], src)
+            return dst
 
         def load_list(name, src):
-            t = tile(name, [P, H // LANES], U16)
-            nc.sync.dma_start(t[:], src)
-            return t
+            return load(name, [P, H // GROUP], U16, src)
 
-        def entries(lst, c0, c1):
-            return lst[:, c0 // LANES : c1 // LANES]
+        def load_scales(plane, src):
+            for q in range(QUADRANTS):
+                nc.sync.dma_start(scale_rows(plane, q), src[0, 4 * q : 4 * q + 4, :].bitcast(I32))
 
-        def load_scales(queue, dst, src):
-            for q in range(4):
-                queue.dma_start(dst[32 * q : 32 * q + 4, :].bitcast(I32), src[0, 4 * q : 4 * q + 4, :].bitcast(I32))
+        def load_tab(t):
+            window = tile("tab%d" % t, [P, WINDOW], F32)
+            nc.sync.dma_start(window[:, :H], dealt(tab)[:, t, :])
+            return window
 
-        def load_words(dst, src):
-            nc.sync.dma_start(dst[:], src[0].rearrange("p n t -> p (n t)").bitcast(I32))
+        def look_up(window, lists, cols):
+            return window[:].indirect(lists[:, cols.start // GROUP : cols.stop // GROUP])
 
-        def deal(name, src, dtype, tag=None):
-            dst = tile(name, [P, S], dtype, tag)
+        def deal_columns(name, src, dtype, after=None):
+            dst = tile(name, [P, S], dtype, after)
             nc.vector.tensor_copy(dst[:].rearrange("p (t m) -> p t m", t=PACK), src.rearrange("p (m t) -> p t m", t=PACK))
             return dst
 
-        def interleave(copy, dst, src):
-            copy(dst.rearrange("p (c i t) -> p c t i", i=4, t=PACK), src.rearrange("p t (c i) -> p c t i", i=4))
+        def interleave(copy, dst, src, cols):
+            copy(
+                dst[:, PACK * cols.start : PACK * cols.stop].rearrange("p (c i t) -> p c t i", i=4, t=PACK),
+                src[:, :, cols].rearrange("p t (c i) -> p c t i", i=4),
+            )
 
-        def shared(dst, src, share):
-            interleave(nc.scalar.copy, dst[:, : PACK * share], src[:, :, :share])
-            interleave(nc.vector.tensor_copy, dst[:, PACK * share :], src[:, :, share:])
+        def quantize(codes, scales, interleaved):
+            nc.vector.quantize_mx(codes.bitcast(FP8X4), scales, interleaved)
+
+        def product(out, t, words, scales, codes, code_scales):
+            rows = slice(t * P, (t + 1) * P)
+            nc.tensor.matmul_mx(
+                out, lhsT=words[:, rows].bitcast(FP8X4), lhsT_scale=scales[:, rows],
+                rhs=codes.bitcast(FP8X4), rhs_scale=code_scales, start=True, stop=True,
+            )
 
         xs_all = tile("xs_all", [P, T], U8)
         nc.vector.memset(xs_all[:, : T // 2].bitcast(I32), 0)
         nc.gpsimd.memset(xs_all[:, T // 2 :].bitcast(I32), 0)
-        warm_in = tile("warm_in", [P, 1], F32, "wa_raw0")
-        warm_out = tile("warm_out", [P, 1], F32, "wa_raw1")
-        nc.vector.memset(warm_in[:], 0.0)
-        nc.scalar.activation(warm_out[:], warm_in[:], ACT.Tanh)
+        ws_raw = tile("ws_raw", [P, N], U8)
+        nc.gpsimd.memset(ws_raw[:].bitcast(I32), 0)
 
         offs_t = load_list("offs_t", offs)
-        n1_t = load_list("n1_t", n1)
-        n2_t = load_list("n2_t", n2)
-        load_scales(nc.sync, xs_all, x_scales)
-        xw_all = tile("xw_all", [P, T], I32)
-        load_words(xw_all, x_words)
         n3_t = load_list("n3_t", n3)
+        tab_t = [load_tab(0)]
+        load_scales(xs_all, x_scales)
+        xw_all = load("xw_all", [P, T], I32, words_of(x_words))
+        wa_raw = [load("wa_raw%d" % a, [P, PACK, HALF], F32, dealt(wa)[:, :, cols]) for a, cols in enumerate(HALVES)]
+        tab_t.append(load_tab(1))
+        load_scales(ws_raw, w1_scales)
+        n1_t = load_list("n1_t", n1)
+        gt_t = load("gt_t", [P, PACK], F32, gt.rearrange("(p t) o -> p (t o)", t=PACK))
+        n2_t = load_list("n2_t", n2)
+        ww_raw = load("ww_raw", [P, N], I32, words_of(w1_words))
+        tab_t.extend([load_tab(2), load_tab(3)])
         n4_t = load_list("n4_t", n4)
-        wa_rows = wa.rearrange("(p j) c -> p j c", j=PACK)
-        wa_raw = [tile("wa_raw%d" % a, [P, PACK, HALF], F32) for a in range(2)]
-        for a in range(2):
-            nc.sync.dma_start(wa_raw[a][:], wa_rows[:, :, a * HALF : (a + 1) * HALF])
 
-        y = [tile("y%d" % t, [P, 2 * H], F32) for t in range(PACK)]
-        def quantize(codes, scales, grouped):
-            nc.vector.quantize_mx(codes.bitcast(FP8X4), scales, grouped)
+        kind = {}
 
-        def product(out, t, words, scales, codes, code_scales):
-            rows = slice(t * P, (t + 1) * P)
-            nc.tensor.matmul_mx(out, lhsT=words[:, rows].bitcast(FP8X4), lhsT_scale=scales[:, rows],
-                                rhs=codes.bitcast(FP8X4), rhs_scale=code_scales, start=True, stop=True)
+        def look_up_tab(t, after=None):
+            kind[t] = tile("kind%d" % t, [P, H], F32, after)
+            nc.vector.tensor_copy(kind[t][:], look_up(tab_t[t], n3_t, WHOLE))
 
-        cols = [slice(0, HALF), slice(HALF, H)]
-        y_ps = [psum.tile([P, H], F32, name="y_ps%d" % t) for t in range(PACK)]
+        look_up_tab(0)
         xs_pick = tile("xs_pick", [P, S], U8)
         nc.vector.tensor_copy(xs_pick[:], xs_all[:].indirect(offs_t[:]))
         xw_pick = tile("xw_pick", [P, S], U32)
         nc.vector.tensor_copy(xw_pick[:], xw_all[:].bitcast(U32).indirect(offs_t[:]))
-        xs = deal("xs", xs_pick[:], U8)
-        xw = deal("xw", xw_pick[:], U32)
+        xs = deal_columns("xs", xs_pick[:], U8)
+        xw = deal_columns("xw", xw_pick[:], U32)
+
         wa_bf = [tile("wa_bf%d" % a, [P, PACK * HALF], BF16) for a in range(2)]
         wa_codes = tile("wa_codes", [P, H], U32)
         wa_scales = tile("wa_scales", [P, H], U8)
-        h_ps = [[psum.tile([P, HALF], F32, name="h_ps%d" % t)[:] for t in range(PACK)], [y_ps[t][:, :HALF] for t in range(PACK)]]
-        y0_ps = [h_ps[0][0], h_ps[1][0]]
-        for a, share in enumerate((128, 64)):
-            shared(wa_bf[a][:], wa_raw[a][:], share)
-            quantize(wa_codes[:, cols[a]], wa_scales[:, cols[a]], wa_bf[a][:])
-            product(y0_ps[a], 0, xw, xs, wa_codes[:, cols[a]], wa_scales[:, cols[a]])
+        interleave(nc.scalar.copy, wa_bf[0], wa_raw[0], slice(0, HALF))
+        interleave(nc.scalar.copy, wa_bf[1], wa_raw[1], slice(0, WA_SCALAR_SHARE))
+        interleave(nc.vector.tensor_copy, wa_bf[1], wa_raw[1], slice(WA_SCALAR_SHARE, HALF))
+
+        wide = [psum.tile([P, H], F32, name="wide%d" % t) for t in range(PACK)]
+        narrow = [psum.tile([P, HALF], F32, name="narrow%d" % t) for t in range(PACK)]
+        half_ps = [[narrow[t][:] for t in range(PACK)], [wide[t][:, :HALF] for t in range(PACK)]]
+        for a, cols in enumerate(HALVES):
+            quantize(wa_codes[:, cols], wa_scales[:, cols], wa_bf[a][:])
+            product(half_ps[a][0], 0, xw, xs, wa_codes[:, cols], wa_scales[:, cols])
         for t in range(1, PACK):
-            product(y_ps[t][:], t, xw, xs, wa_codes[:], wa_scales[:])
+            product(wide[t][:], t, xw, xs, wa_codes[:], wa_scales[:])
 
-        gt_t = tile("gt_t", [P, PACK], F32, "xs_pick")
-        nc.sync.dma_start(gt_t[:], gt.rearrange("(p t) o -> p (t o)", t=PACK))
-        ww_raw = tile("ww_raw", [P, N], I32, "xw_all")
-        load_words(ww_raw, w1_words)
-        ws_raw = tile("ws_raw", [P, N], U8, "xs_all")
-        nc.gpsimd.memset(ws_raw[:].bitcast(I32), 0)
-        load_scales(nc.sync, ws_raw, w1_scales)
-        ww = deal("ww", ww_raw[:].bitcast(U32), U32, "wa_bf1")
-        tab_rows = tab.rearrange("(p t) c -> p t c", t=PACK)
-        tab_t = []
-        for t, tag in enumerate(("wa_raw0", "wa_raw1", "wa_bf0", "xw_all")):
-            rows = tile("tab%d" % t, [P, 2 * J], F32, tag)
-            nc.sync.dma_start(rows[:, :J], tab_rows[:, t, :])
-            tab_t.append(rows)
+        look_up_tab(1, after="wa_bf1")
+        ws = deal_columns("ws", ws_raw[:], U8, after="tab1")
 
-        gy = [tile("gy%d" % t, [P, 2 * H], F32) for t in range(PACK)]
+        y = [tile("y%d" % t, [P, WINDOW], F32) for t in range(PACK)]
+        gy = [tile("gy%d" % t, [P, WINDOW], F32) for t in range(PACK)]
         diff = [tile("diff%d" % t, [P, H], F32) for t in range(PACK)]
         th = [tile("th%d" % t, [P, H], F32) for t in range(PACK)]
         z = tile("z", [P, PACK, H], F32)
 
-        def Y(t):
-            nc.scalar.copy(y[t][:, :H], y_ps[t][:])
+        def y_in_psum(t, cols):
+            return wide[t][:] if cols == WHOLE else half_ps[cols.start // HALF][t]
 
-        def O(t):
-            nc.scalar.copy(gy[t][:, H:], y_ps[t][:])
+        def copy_window(t, cols):
+            nc.scalar.copy(y[t][:, cols], y_in_psum(t, cols))
 
-        def G(t):
-            nc.scalar.activation(gy[t][:, :H], y_ps[t][:], ACT.Copy, scale=gt_t[:, t : t + 1])
+        def difference(t, cols):
+            plain = gy[t][:, H:][:, cols]
+            nc.scalar.copy(plain, y_in_psum(t, cols))
+            return lambda: nc.vector.tensor_tensor(diff[t][:, cols], look_up(y[t], n1_t, cols), plain, ALU.subtract)
 
-        def D(t, c0=0, c1=H):
-            nc.vector.tensor_tensor(diff[t][:, c0:c1], y[t][:].indirect(entries(n1_t, c0, c1)), gy[t][:, H + c0 : H + c1], ALU.subtract)
+        def weigh(t, cols):
+            nc.scalar.activation(gy[t][:, cols], y_in_psum(t, cols), ACT.Copy, scale=gt_t[:, t : t + 1])
 
-        def TH(t, c0=0, c1=H):
-            nc.scalar.activation(th[t][:, c0:c1], diff[t][:, c0:c1], ACT.Tanh)
+        def squash(t, cols):
+            nc.scalar.activation(th[t][:, cols], diff[t][:, cols], ACT.Tanh)
 
-        def M(t, c0=0, c1=H):
-            nc.vector.tensor_tensor(z[:, t, c0:c1], gy[t][:].indirect(entries(n2_t, c0, c1)), th[t][:, c0:c1], ALU.mult)
+        def multiply(t, cols):
+            nc.vector.tensor_tensor(z[:, t, cols], look_up(gy[t], n2_t, cols), th[t][:, cols], ALU.mult)
 
-        nc.scalar.copy(y[0][:, :HALF], y0_ps[0])
-        nc.scalar.copy(gy[0][:, H : H + HALF], y0_ps[0])
-        nc.scalar.copy(y[0][:, HALF:H], y0_ps[1])
-        D(0, 0, HALF)
-        nc.scalar.copy(gy[0][:, H + HALF :], y0_ps[1])
-        D(0, HALF, H)
-        Y(1); O(1); D(1)
-        for a in range(2):
-            nc.scalar.activation(gy[0][:, cols[a]], y0_ps[a], ACT.Copy, scale=gt_t[:, 0:1])
-        TH(0)
-        ws = deal("ws", ws_raw[:], U8, "diff0")
-        M(0); G(1); TH(1); M(1); Y(2); O(2); D(2); Y(3); O(3); D(3); G(2)
-        TH(2, 0, HALF); M(2, 0, HALF); G(3); TH(2, HALF, H); TH(3, 0, HALF); M(3, 0, HALF); TH(3, HALF, H)
+        copy_window(0, HALVES[0])
+        subtract = difference(0, HALVES[0])
+        copy_window(0, HALVES[1])
+        subtract()
+        difference(0, HALVES[1])()
+        copy_window(1, WHOLE)
+        difference(1, WHOLE)()
+        for cols in HALVES:
+            weigh(0, cols)
+        squash(0, WHOLE)
+        multiply(0, WHOLE)
+        weigh(1, WHOLE)
+        squash(1, WHOLE)
+        ww = deal_columns("ww", ww_raw[:].bitcast(U32), U32, after="diff1")
+        multiply(1, WHOLE)
+        for t in (2, 3):
+            copy_window(t, WHOLE)
+            difference(t, WHOLE)()
+        weigh(2, WHOLE)
+        squash(2, HALVES[0])
+        multiply(2, HALVES[0])
+        weigh(3, WHOLE)
+        squash(2, HALVES[1])
+        squash(3, HALVES[0])
+        multiply(3, HALVES[0])
+        squash(3, HALVES[1])
         z_bf = [tile("z_bf%d" % a, [P, PACK * HALF], BF16) for a in range(2)]
-        interleave(nc.scalar.copy, z_bf[0][:], z[:, :, cols[0]])
-        M(2, HALF, H); M(3, HALF, H)
+        interleave(nc.scalar.copy, z_bf[0], z[:, :, HALVES[0]], slice(0, HALF))
+        for t in (2, 3):
+            multiply(t, HALVES[1])
 
         def second_product(a):
             z_codes = tile("z_codes%d" % a, [P, HALF], U32)
             z_scales = tile("z_scales%d" % a, [P, HALF], U8)
             quantize(z_codes[:], z_scales[:], z_bf[a][:])
             for t in range(PACK):
-                product(h_ps[a][t], t, ww, ws, z_codes[:], z_scales[:])
-
-        h = y
-
-        def HC(t, a):
-            nc.scalar.copy(h[t][:, cols[a]], h_ps[a][t])
+                product(half_ps[a][t], t, ww, ws, z_codes[:], z_scales[:])
 
         second_product(0)
-        shared(z_bf[1][:], z[:, :, cols[1]], 96)
+        interleave(nc.scalar.copy, z_bf[1], z[:, :, HALVES[1]], slice(0, HALF))
+        look_up_tab(2, after="th3")
         second_product(1)
-        HC(0, 0); HC(1, 0); HC(0, 1); HC(1, 1); HC(2, 0); HC(2, 1); HC(3, 0); HC(3, 1)
+        look_up_tab(3, after="z_bf1")
 
-        out_rows = out_0.rearrange("(p t) c -> p t c", t=PACK)
-        out_words = out_1[0].rearrange("p n t -> p (n t)").bitcast(I32)
-        o_codes = tile("o_codes", [P, H], I32)
-        o_scales = tile("o_scales", [P, H], U8)
+        h = y
+        for t, a in [(t, a) for a in range(2) for t in (0, 1)] + [(t, a) for t in (2, 3) for a in range(2)]:
+            nc.scalar.copy(h[t][:, HALVES[a]], half_ps[a][t])
+
         first = tile("first", [P, PACK, H], F32)
         second = tile("second", [P, PACK, H], F32)
         res = tile("res", [P, PACK, H], F32)
         res_bf = tile("res_bf", [P, PACK * H], BF16)
+        o_codes = tile("o_codes", [P, H], I32)
+        o_scales = tile("o_scales", [P, H], U8)
 
-        def A(t, c0=0, c1=H):
-            nc.vector.tensor_tensor(first[:, t, c0:c1], tab_t[t][:].indirect(entries(n3_t, c0, c1)), h[t][:, c0:c1], ALU.add)
+        for t, cols in [(t, cols) for cols in HALVES for t in (0, 1)] + [(2, WHOLE), (3, WHOLE)]:
+            nc.gpsimd.tensor_tensor(first[:, t, cols], kind[t][:, cols], h[t][:, cols], ALU.add)
+        for t in range(PACK):
+            nc.vector.tensor_copy(second[:, t, :], look_up(h[t], n4_t, WHOLE))
 
-        def B(t, c0=0, c1=H):
-            nc.vector.tensor_copy(second[:, t, c0:c1], h[t][:].indirect(entries(n4_t, c0, c1)))
+        def larger(tiles, cols):
+            nc.vector.tensor_tensor(res[:, tiles, cols], first[:, tiles, cols], second[:, tiles, cols], ALU.max)
 
-        def X(t0, t1, c0=0, c1=H):
-            nc.vector.tensor_tensor(res[:, t0:t1, c0:c1], first[:, t0:t1, c0:c1], second[:, t0:t1, c0:c1], ALU.max)
-            nc.sync.dma_start(out_rows[:, t0:t1, c0:c1], res[:, t0:t1, c0:c1])
+        def store_result(cols):
+            nc.sync.dma_start(dealt(out_0)[:, :, cols], res[:, :, cols])
 
-        def Q(c0, c1):
-            nc.vector.quantize_mx(o_codes[:, c0:c1].bitcast(FP8X4), o_scales[:, c0:c1], res_bf[:, PACK * c0 : PACK * c1])
-            nc.sync.dma_start(out_words[:, c0:c1], o_codes[:, c0:c1])
+        def quantize_result(cols):
+            quantize(o_codes[:, cols], o_scales[:, cols], res_bf[:, PACK * cols.start : PACK * cols.stop])
 
-        A(0, 0, HALF); A(1, 0, HALF); B(0); A(0, HALF, H); A(1, HALF, H); B(1); X(0, 1); A(2); X(1, 2); A(3)
-        B(2, 0, HALF); B(3, 0, HALF); B(2, HALF, H); X(2, 4, 0, HALF)
-        interleave(nc.scalar.copy, res_bf[:, : PACK * HALF], res[:, :, :HALF])
-        B(3, HALF, H); X(2, 3, HALF, H); X(3, 4, HALF, H); Q(0, HALF)
-        shared(res_bf[:, PACK * HALF :], res[:, :, HALF:], 64)
-        Q(HALF, H)
-        for q in range(4):
+        def store_words(cols):
+            nc.sync.dma_start(words_of(out_1)[:, cols], o_codes[:, cols])
+
+        larger(slice(0, PACK - 1), QUARTERS[0])
+        larger(slice(PACK - 1, PACK), QUARTERS[0])
+        interleave(nc.scalar.copy, res_bf, res, QUARTERS[0])
+        larger(slice(0, PACK), QUARTERS[1])
+        store_result(HALVES[0])
+        interleave(nc.scalar.copy, res_bf, res, QUARTERS[1])
+        larger(slice(0, PACK), QUARTERS[2])
+        store_result(QUARTERS[2])
+        interleave(nc.scalar.copy, res_bf, res, QUARTERS[2])
+        larger(slice(0, PACK), QUARTERS[3])
+        store_result(QUARTERS[3])
+        quantize_result(HALVES[0])
+        store_words(HALVES[0])
+        interleave(nc.vector.tensor_copy, res_bf, res, QUARTERS[3])
+        quantize_result(QUARTERS[2])
+        quantize_result(QUARTERS[3])
+        store_words(HALVES[1])
+        for q in range(QUADRANTS):
             queue = nc.scalar if q % 2 else nc.sync
-            queue.dma_start(out_2[0, 4 * q : 4 * q + 4, :].bitcast(I32), o_scales[32 * q : 32 * q + 4, :].bitcast(I32))
+            queue.dma_start(out_2[0, 4 * q : 4 * q + 4, :].bitcast(I32), scale_rows(o_scales, q))

@@ -24,7 +24,7 @@ HALF, QUARTER = H // 2, H // 4
 HALVES = (slice(0, HALF), slice(HALF, H))
 QUARTERS = tuple(slice(c, c + QUARTER) for c in range(0, H, QUARTER))
 WHOLE = slice(0, H)
-WA_SCALAR_SHARE = 64
+WA_SCALAR_SHARES = (160, 96)
 
 
 def tile_picked_tokfdifkind_none_po_kernel(
@@ -126,14 +126,13 @@ def tile_picked_tokfdifkind_none_po_kernel(
         wa_bf = [tile("wa_bf%d" % a, [P, PACK * HALF], BF16) for a in range(2)]
         wa_codes = tile("wa_codes", [P, H], U32)
         wa_scales = tile("wa_scales", [P, H], U8)
-        interleave(nc.scalar.copy, wa_bf[0], wa_raw[0], slice(0, HALF))
-        interleave(nc.scalar.copy, wa_bf[1], wa_raw[1], slice(0, WA_SCALAR_SHARE))
-        interleave(nc.vector.tensor_copy, wa_bf[1], wa_raw[1], slice(WA_SCALAR_SHARE, HALF))
 
         wide = [psum.tile([P, H], F32, name="wide%d" % t) for t in range(PACK)]
         narrow = [psum.tile([P, HALF], F32, name="narrow%d" % t) for t in range(PACK)]
         half_ps = [[narrow[t][:] for t in range(PACK)], [wide[t][:, :HALF] for t in range(PACK)]]
         for a, cols in enumerate(HALVES):
+            interleave(nc.scalar.copy, wa_bf[a], wa_raw[a], slice(0, WA_SCALAR_SHARES[a]))
+            interleave(nc.vector.tensor_copy, wa_bf[a], wa_raw[a], slice(WA_SCALAR_SHARES[a], HALF))
             quantize(wa_codes[:, cols], wa_scales[:, cols], wa_bf[a][:])
             product(half_ps[a][0], 0, xw, xs, wa_codes[:, cols], wa_scales[:, cols])
         for t in range(1, PACK):

from contextlib import ExitStack

import concourse.mybir as mybir

K, T, S, N, H = 512, 2048, 512, 512, 512
FLOPS = 2 * K * S * H + 2 * S * N * H

F32 = mybir.dt.float32
BF16 = mybir.dt.bfloat16
I32 = mybir.dt.int32
U32 = mybir.dt.uint32
U16 = mybir.dt.uint16
U8 = mybir.dt.uint8
FP8X4 = mybir.dt.float8_e4m3fn_x4
ALU = mybir.AluOpType
ACT = mybir.ActivationFunctionType

P = 128
PACK = 4
GROUP = 16
QUADRANTS = 4
WINDOW = 2 * H
HALF, QUARTER = H // 2, H // 4
HALVES = (slice(0, HALF), slice(HALF, H))
QUARTERS = tuple(slice(c, c + QUARTER) for c in range(0, H, QUARTER))
WHOLE = slice(0, H)
WA_SCALAR_SHARES = (160, 96)


def tile_picked_tokfdifkind_none_po_kernel(
    tc, x_words, x_scales, wa, gt, w1_words, w1_scales, tab, offs, n1, n2, n3, n4, out_0, out_1, out_2
):
    nc = tc.nc
    with ExitStack() as ctx:
        keep = ctx.enter_context(tc.tile_pool(name="keep", bufs=1))
        psum = ctx.enter_context(tc.psum_pool(name="psum", bufs=1))

        def tile(name, shape, dtype, after=None):
            return keep.tile(shape, dtype, name=name, tag=after or name, align_bytes=64)

        def dealt(rows):
            return rows.rearrange("(p t) c -> p t c", t=PACK)

        def words_of(packed):
            return packed[0].rearrange("p n t -> p (n t)").bitcast(I32)

        def scale_rows(plane, q):
            return plane[32 * q : 32 * q + 4, :].bitcast(I32)

        def load(name, shape, dtype, src):
            dst = tile(name, shape, dtype)
            nc.sync.dma_start(dst[:], src)
            return dst

        def load_list(name, src):
            return load(name, [P, H // GROUP], U16, src)

        def load_scales(plane, src):
            for q in range(QUADRANTS):
                nc.sync.dma_start(scale_rows(plane, q), src[0, 4 * q : 4 * q + 4, :].bitcast(I32))

        def load_tab(t):
            window = tile("tab%d" % t, [P, WINDOW], F32)
            nc.sync.dma_start(window[:, :H], dealt(tab)[:, t, :])
            return window

        def look_up(window, lists, cols):
            return window[:].indirect(lists[:, cols.start // GROUP : cols.stop // GROUP])

        def deal_columns(name, src, dtype, after=None):
            dst = tile(name, [P, S], dtype, after)
            nc.vector.tensor_copy(dst[:].rearrange("p (t m) -> p t m", t=PACK), src.rearrange("p (m t) -> p t m", t=PACK))
            return dst

        def interleave(copy, dst, src, cols):
            copy(
                dst[:, PACK * cols.start : PACK * cols.stop].rearrange("p (c i t) -> p c t i", i=4, t=PACK),
                src[:, :, cols].rearrange("p t (c i) -> p c t i", i=4),
            )

        def quantize(codes, scales, interleaved):
            nc.vector.quantize_mx(codes.bitcast(FP8X4), scales, interleaved)

        def product(out, t, words, scales, codes, code_scales):
            rows = slice(t * P, (t + 1) * P)
            nc.tensor.matmul_mx(
                out, lhsT=words[:, rows].bitcast(FP8X4), lhsT_scale=scales[:, rows],
                rhs=codes.bitcast(FP8X4), rhs_scale=code_scales, start=True, stop=True,
            )

        xs_all = tile("xs_all", [P, T], U8)
        nc.vector.memset(xs_all[:, : T // 2].bitcast(I32), 0)
        nc.gpsimd.memset(xs_all[:, T // 2 :].bitcast(I32), 0)
        ws_raw = tile("ws_raw", [P, N], U8)
        nc.gpsimd.memset(ws_raw[:].bitcast(I32), 0)

        offs_t = load_list("offs_t", offs)
        n3_t = load_list("n3_t", n3)
        tab_t = [load_tab(0)]
        load_scales(xs_all, x_scales)
        xw_all = load("xw_all", [P, T], I32, words_of(x_words))
        wa_raw = [load("wa_raw%d" % a, [P, PACK, HALF], F32, dealt(wa)[:, :, cols]) for a, cols in enumerate(HALVES)]
        tab_t.append(load_tab(1))
        load_scales(ws_raw, w1_scales)
        n1_t = load_list("n1_t", n1)
        gt_t = load("gt_t", [P, PACK], F32, gt.rearrange("(p t) o -> p (t o)", t=PACK))
        n2_t = load_list("n2_t", n2)
        ww_raw = load("ww_raw", [P, N], I32, words_of(w1_words))
        tab_t.extend([load_tab(2), load_tab(3)])
        n4_t = load_list("n4_t", n4)

        kind = {}

        def look_up_tab(t, after=None):
            kind[t] = tile("kind%d" % t, [P, H], F32, after)
            nc.vector.tensor_copy(kind[t][:], look_up(tab_t[t], n3_t, WHOLE))

        look_up_tab(0)
        xs_pick = tile("xs_pick", [P, S], U8)
        nc.vector.tensor_copy(xs_pick[:], xs_all[:].indirect(offs_t[:]))
        xw_pick = tile("xw_pick", [P, S], U32)
        nc.vector.tensor_copy(xw_pick[:], xw_all[:].bitcast(U32).indirect(offs_t[:]))
        xs = deal_columns("xs", xs_pick[:], U8)
        xw = deal_columns("xw", xw_pick[:], U32)

        wa_bf = [tile("wa_bf%d" % a, [P, PACK * HALF], BF16) for a in range(2)]
        wa_codes = tile("wa_codes", [P, H], U32)
        wa_scales = tile("wa_scales", [P, H], U8)

        wide = [psum.tile([P, H], F32, name="wide%d" % t) for t in range(PACK)]
        narrow = [psum.tile([P, HALF], F32, name="narrow%d" % t) for t in range(PACK)]
        half_ps = [[narrow[t][:] for t in range(PACK)], [wide[t][:, :HALF] for t in range(PACK)]]
        for a, cols in enumerate(HALVES):
            interleave(nc.scalar.copy, wa_bf[a], wa_raw[a], slice(0, WA_SCALAR_SHARES[a]))
            interleave(nc.vector.tensor_copy, wa_bf[a], wa_raw[a], slice(WA_SCALAR_SHARES[a], HALF))
            quantize(wa_codes[:, cols], wa_scales[:, cols], wa_bf[a][:])
            product(half_ps[a][0], 0, xw, xs, wa_codes[:, cols], wa_scales[:, cols])
        for t in range(1, PACK):
            product(wide[t][:], t, xw, xs, wa_codes[:], wa_scales[:])

        look_up_tab(1, after="wa_bf1")
        ws = deal_columns("ws", ws_raw[:], U8, after="tab1")

        y = [tile("y%d" % t, [P, WINDOW], F32) for t in range(PACK)]
        gy = [tile("gy%d" % t, [P, WINDOW], F32) for t in range(PACK)]
        diff = [tile("diff%d" % t, [P, H], F32) for t in range(PACK)]
        th = [tile("th%d" % t, [P, H], F32) for t in range(PACK)]
        z = tile("z", [P, PACK, H], F32)

        def y_in_psum(t, cols):
            return wide[t][:] if cols == WHOLE else half_ps[cols.start // HALF][t]

        def copy_window(t, cols):
            nc.scalar.copy(y[t][:, cols], y_in_psum(t, cols))

        def difference(t, cols):
            plain = gy[t][:, H:][:, cols]
            nc.scalar.copy(plain, y_in_psum(t, cols))
            return lambda: nc.vector.tensor_tensor(diff[t][:, cols], look_up(y[t], n1_t, cols), plain, ALU.subtract)

        def weigh(t, cols):
            nc.scalar.activation(gy[t][:, cols], y_in_psum(t, cols), ACT.Copy, scale=gt_t[:, t : t + 1])

        def squash(t, cols):
            nc.scalar.activation(th[t][:, cols], diff[t][:, cols], ACT.Tanh)

        def multiply(t, cols):
            nc.vector.tensor_tensor(z[:, t, cols], look_up(gy[t], n2_t, cols), th[t][:, cols], ALU.mult)

        copy_window(0, HALVES[0])
        subtract = difference(0, HALVES[0])
        copy_window(0, HALVES[1])
        subtract()
        difference(0, HALVES[1])()
        copy_window(1, WHOLE)
        difference(1, WHOLE)()
        for cols in HALVES:
            weigh(0, cols)
        squash(0, WHOLE)
        multiply(0, WHOLE)
        weigh(1, WHOLE)
        squash(1, WHOLE)
        ww = deal_columns("ww", ww_raw[:].bitcast(U32), U32, after="diff1")
        multiply(1, WHOLE)
        for t in (2, 3):
            copy_window(t, WHOLE)
            difference(t, WHOLE)()
        weigh(2, WHOLE)
        squash(2, HALVES[0])
        multiply(2, HALVES[0])
        weigh(3, WHOLE)
        squash(2, HALVES[1])
        squash(3, HALVES[0])
        multiply(3, HALVES[0])
        squash(3, HALVES[1])
        z_bf = [tile("z_bf%d" % a, [P, PACK * HALF], BF16) for a in range(2)]
        interleave(nc.scalar.copy, z_bf[0], z[:, :, HALVES[0]], slice(0, HALF))
        for t in (2, 3):
            multiply(t, HALVES[1])

        def second_product(a):
            z_codes = tile("z_codes%d" % a, [P, HALF], U32)
            z_scales = tile("z_scales%d" % a, [P, HALF], U8)
            quantize(z_codes[:], z_scales[:], z_bf[a][:])
            for t in range(PACK):
                product(half_ps[a][t], t, ww, ws, z_codes[:], z_scales[:])

        second_product(0)
        interleave(nc.scalar.copy, z_bf[1], z[:, :, HALVES[1]], slice(0, HALF))
        look_up_tab(2, after="th3")
        second_product(1)
        look_up_tab(3, after="z_bf1")

        h = y
        for t, a in [(t, a) for a in range(2) for t in (0, 1)] + [(t, a) for t in (2, 3) for a in range(2)]:
            nc.scalar.copy(h[t][:, HALVES[a]], half_ps[a][t])

        first = tile("first", [P, PACK, H], F32)
        second = tile("second", [P, PACK, H], F32)
        res = tile("res", [P, PACK, H], F32)
        res_bf = tile("res_bf", [P, PACK * H], BF16)
        o_codes = tile("o_codes", [P, H], I32)
        o_scales = tile("o_scales", [P, H], U8)

        for t, cols in [(t, cols) for cols in HALVES for t in (0, 1)] + [(2, WHOLE), (3, WHOLE)]:
            nc.gpsimd.tensor_tensor(first[:, t, cols], kind[t][:, cols], h[t][:, cols], ALU.add)
        for t in range(PACK):
            nc.vector.tensor_copy(second[:, t, :], look_up(h[t], n4_t, WHOLE))

        def larger(tiles, cols):
            nc.vector.tensor_tensor(res[:, tiles, cols], first[:, tiles, cols], second[:, tiles, cols], ALU.max)

        def store_result(cols):
            nc.sync.dma_start(dealt(out_0)[:, :, cols], res[:, :, cols])

        def quantize_result(cols):
            quantize(o_codes[:, cols], o_scales[:, cols], res_bf[:, PACK * cols.start : PACK * cols.stop])

        def store_words(cols):
            nc.sync.dma_start(words_of(out_1)[:, cols], o_codes[:, cols])

        larger(slice(0, PACK - 1), QUARTERS[0])
        larger(slice(PACK - 1, PACK), QUARTERS[0])
        interleave(nc.scalar.copy, res_bf, res, QUARTERS[0])
        larger(slice(0, PACK), QUARTERS[1])
        store_result(HALVES[0])
        interleave(nc.scalar.copy, res_bf, res, QUARTERS[1])
        larger(slice(0, PACK), QUARTERS[2])
        store_result(QUARTERS[2])
        interleave(nc.scalar.copy, res_bf, res, QUARTERS[2])
        larger(slice(0, PACK), QUARTERS[3])
        store_result(QUARTERS[3])
        quantize_result(HALVES[0])
        store_words(HALVES[0])
        interleave(nc.vector.tensor_copy, res_bf, res, QUARTERS[3])
        quantize_result(QUARTERS[2])
        quantize_result(QUARTERS[3])
        store_words(HALVES[1])
        for q in range(QUADRANTS):
            queue = nc.scalar if q % 2 else nc.sync
            queue.dma_start(out_2[0, 4 * q : 4 * q + 4, :].bitcast(I32), scale_rows(o_scales, q))
